import numpy as np
import ml_dtypes


def mxq(x, axis, fmt="e4m3"):
    dtype, down = {"e4m3": (ml_dtypes.float8_e4m3fn, 7), "e5m2": (ml_dtypes.float8_e5m2, 14)}[fmt]
    v = np.moveaxis(np.asarray(x, np.float32).astype(ml_dtypes.bfloat16).astype(np.float64), axis, -1)
    blocks = v.reshape(v.shape[:-1] + (-1, 32))
    amax = np.abs(blocks).max(-1, keepdims=True)
    byte = np.maximum(np.where(amax > 0, np.frexp(amax)[1] - 1 + 127, 0) - down, 1)
    scale = np.exp2(byte - 127.0)
    codes = (blocks / scale).astype(np.float32).astype(dtype).astype(np.float64)
    return np.moveaxis((codes * scale).reshape(v.shape), -1, axis)


WIDE = False


def mx_kscale(k):
    if not WIDE:
        return np.ones(k)
    levels = np.array([10, -10, 5, -5, 0])
    if k % 512:
        return np.exp2(np.random.permutation(np.resize(levels, k // 32))).repeat(32)
    a = np.empty((k // 512, 16))
    for p in range(k // 512):
        a[p, :8] = np.random.permutation(np.resize(levels, 8))
        for g in range(8):
            far = levels[np.abs(levels - a[p, g]) >= 10]
            a[p, g + 8] = far[np.random.randint(len(far))]
    return np.exp2(a.ravel()).repeat(32)


BF16 = ml_dtypes.bfloat16


def bf(x):
    return np.asarray(x, np.float32).astype(BF16)


def f64(x):
    return np.asarray(x).astype(np.float64)


E2M1 = np.array([0.0, 0.5, 1.0, 1.5, 2.0, 3.0, 4.0, 6.0, -0.0, -0.5, -1.0, -1.5, -2.0, -3.0, -4.0, -6.0])


def pack_weight(w, fmt):
    k, n = w.shape
    w = f64(bf(w)).reshape(k // 32, 32, n)
    amax = np.abs(w).max(1)
    if fmt == "e4m3":
        byte = np.frexp(amax)[1] - 1 + 127 - 7
    else:
        mant, ex = np.frexp(amax / 6.0)
        byte = np.where(mant > 0.5, ex, ex - 1) + 127
    byte = np.clip(np.where(amax > 0, byte, 1), 1, 254)
    scaled = (w * np.exp2(127.0 - byte)[:, None, :]).reshape(k, n).astype(np.float32)
    by_word = np.ascontiguousarray(scaled.reshape(k // 512, 128, 4, n).transpose(0, 1, 3, 2))
    if fmt == "e4m3":
        words = by_word.astype(ml_dtypes.float8_e4m3fn).view(np.uint8)
    else:
        c = by_word.astype(ml_dtypes.float4_e2m1fn).view(np.uint8) & 0xF
        words = c[..., 0::2] | (c[..., 1::2] << 4)
    return np.ascontiguousarray(words), np.ascontiguousarray(byte.astype(np.uint8).reshape(k // 512, 16, n))


def unpack_weight(words, scales, fmt):
    g, p, n, _ = words.shape
    if fmt == "e4m3":
        vals = np.ascontiguousarray(words).view(ml_dtypes.float8_e4m3fn).astype(np.float64)
    else:
        nib = np.empty((g, p, n, 4), np.uint8)
        nib[..., 0::2] = words & 0xF
        nib[..., 1::2] = words >> 4
        vals = E2M1[nib]
    vals = vals * np.repeat(np.exp2(scales.astype(np.float64) - 127.0), 8, axis=1)[..., None]
    return vals.transpose(0, 1, 3, 2).reshape(g * 512, n)
def pack4(w):
    words, scales = pack_weight(w, "e2m1")
    return words.reshape(words.shape[0], 128, -1), scales


def unpack4(words, scales):
    return unpack_weight(words.reshape(words.shape[0], 128, -1, 2), scales, "e2m1")


G, K, L, T, F = 4, 512, 1024, 256, 1024


def setup_inputs():
    s, t = mx_kscale(K), mx_kscale(L)
    a = 2 * np.pi * ((np.arange(K)[:, None] + np.random.uniform(-0.5, 0.5, (G, K, 1))) * np.arange(T) / K
                     + np.random.uniform(0, 1, (G, K, 1)))
    b = 2 * np.pi * ((np.arange(L)[:, None] + np.random.uniform(-0.5, 0.5, (G, L, 1))) * np.arange(F) / L
                     + np.random.uniform(0, 1, (G, L, 1)))
    dop = np.concatenate([np.cos(a), np.sin(a)], axis=2) * np.sqrt(2 / K) / s[:, None]
    dly = np.concatenate([np.cos(b), np.sin(b)], axis=2) / np.sqrt(L) / t[:, None]
    doppler_words, doppler_scales = pack4(dop.reshape(G * K, 2 * T))
    delay_words, delay_scales = pack4(dly.reshape(G * L, 2 * F))
    return {"x": bf(np.random.standard_normal((G, K, L)) * s[:, None] * t),
            "doppler_words": doppler_words, "doppler_scales": doppler_scales,
            "window": bf(1 + 0.1 * np.random.standard_normal((G, 2 * T))),
            "delay_words": delay_words, "delay_scales": delay_scales}


def reference(x, doppler_words, doppler_scales, window, delay_words, delay_scales):
    dop = unpack4(doppler_words, doppler_scales).reshape(G, K, 2 * T)
    dly = unpack4(delay_words, delay_scales).reshape(G, L, 2 * F)
    h = dop.swapaxes(1, 2) @ mxq(f64(x), 1, "e4m3")
    h = h * f64(window)[:, :, None]
    hq = mxq(h, 2, "e4m3")
    c = hq[:, :T] @ dly[:, :, :F]
    d = hq[:, T:] @ dly[:, :, F:]
    return c - d

@@ -1,0 +1,288 @@
+from contextlib import ExitStack
+
+import concourse.mybir as mybir
+from concourse.masks import make_identity
+
+G, K, L, T, F = 4, 512, 1024, 256, 1024
+FLOPS = 2 * G * (2 * T * K * L + T * F * 2 * L)
+
+F32 = mybir.dt.float32
+BF16 = mybir.dt.bfloat16
+U32 = mybir.dt.uint32
+I32 = mybir.dt.int32
+U8 = mybir.dt.uint8
+E4M3 = mybir.dt.float8_e4m3fn_x4
+E2M1 = mybir.dt.float4_e2m1fn_x4
+MULT = mybir.AluOpType.mult
+
+P = 128
+UNITS = 2 * G
+
+
+def tile_real_delay_doppler_expansion_s14_kernel(
+    tc, x, doppler_words, doppler_scales, window, delay_words, delay_scales, out
+):
+    nc = tc.nc
+    with ExitStack() as ctx:
+        keep = ctx.enter_context(tc.tile_pool(name="keep", bufs=1))
+        work = ctx.enter_context(tc.tile_pool(name="work", bufs=3))
+        psum = ctx.enter_context(tc.psum_pool(name="psum", bufs=1))
+        ctx.enter_context(tc.manual_schedule())
+
+        raw = []
+        for u in range(UNITS):
+            if u < 4:
+                raw_half = keep.tile([P, 4, 512], BF16, name="raw%d" % u, align_bytes=64)
+                raw.append((raw_half, 0))
+            elif u % 2 == 0:
+                raw_band = keep.tile([P, 4, L], BF16, name="raw%d" % u, align_bytes=64)
+                raw.append((raw_band, 0))
+                raw.append((raw_band, 512))
+        dop = keep.tile([P, G, 4 * T], U8, name="dop", align_bytes=64)
+        dop_s = keep.tile([P, G, 2 * T], U8, name="dop_s", align_bytes=64)
+        dly = [keep.tile([P, 2, 4 * F], U8, name="dly%d" % b, align_bytes=64) for b in range(G)]
+        dly_s = [keep.tile([P, 2, 2 * F], U8, name="dly_s%d" % b, align_bytes=64) for b in range(G)]
+        res = [keep.tile([P, 2, F], F32, name="res%d" % b, align_bytes=64) for b in range(G)]
+        ident = keep.tile([P, P], F32, name="ident", align_bytes=64)
+        wrow = keep.tile([P, P], F32, name="wrow", align_bytes=64)
+        wcol = keep.tile([P, 2 * G], F32, name="wcol", align_bytes=64)
+        gain = keep.tile([P, G * T], F32, name="gain", align_bytes=64)
+        dummy = keep.tile([P, 2], BF16, name="dummy", align_bytes=64)
+
+        nc.vector.memset(wrow[:], 0.0)
+        nc.vector.memset(dop_s[:].rearrange("p g n -> p (g n)").bitcast(I32), 0)
+        nc.vector.memset(dummy[:], 0.0)
+        nc.vector.memset(dly_s[0][:].rearrange("p g n -> p (g n)").bitcast(I32), 0)
+        make_identity(nc, ident[:])
+        for b in range(1, G):
+            nc.gpsimd.memset(dly_s[b][:].rearrange("p g n -> p (g n)").bitcast(I32), 0)
+
+        nc.scalar.dma_start(
+            out=wrow[0 : 2 * G, :],
+            in_=window.bitcast(F32).rearrange("b (h n) -> (b h) n", h=2),
+        )
+        ds = doppler_scales.bitcast(I32).rearrange("g (q r) n -> r q g n", r=4)
+        for r in range(4):
+            nc.scalar.dma_start(out=dop_s[r:P:32, :, :].bitcast(I32), in_=ds[r])
+        nc.scalar.copy(out=dummy[:, 1:2], in_=dummy[:, 0:1])
+
+        def load_x(u):
+            tile, c0 = raw[u]
+            b = u // 2
+            if u < 4:
+                src = x[b][:, 512 * (u % 2) : 512 * (u % 2) + 512]
+            else:
+                src = x[b]
+            nc.sync.dma_start(out=tile[:], in_=src.rearrange("(p j) l -> p j l", j=4))
+
+        def load_dop(b0):
+            nc.sync.dma_start(
+                out=dop[:, b0 : b0 + 2, :],
+                in_=doppler_words[b0 : b0 + 2].rearrange("g p c -> p g c"),
+            )
+
+        def load_dly(b, g):
+            nc.sync.dma_start(out=dly[b][:, g, :], in_=delay_words[2 * b + g])
+
+        def load_dly_s(b):
+            src = delay_scales[2 * b : 2 * b + 2].bitcast(I32).rearrange("g (q r) n -> r q g n", r=4)
+            for r in range(4):
+                nc.sync.dma_start(out=dly_s[b][r:P:32, :, :].bitcast(I32), in_=src[r])
+
+        load_x(0)
+        load_dop(0)
+        load_x(1)
+        load_x(2)
+        load_dly_s(0)
+        load_dly(0, 0)
+        load_x(3)
+        load_dly(0, 1)
+        load_dop(2)
+        load_x(4)
+        load_dly_s(1)
+        load_dly(1, 0)
+        load_dly(1, 1)
+        load_x(6)
+        load_dly_s(2)
+        load_dly(2, 0)
+        load_dly(2, 1)
+        load_dly_s(3)
+        load_dly(3, 0)
+        load_dly(3, 1)
+
+        xi = {}
+        xq = {}
+        v = {}
+        vq = {}
+        hb = {}
+        ob = {}
+
+        def interleave(u, t0, t1, copy):
+            tile, c0 = raw[u]
+            if u not in xi:
+                xi_tile = work.tile([P, 2048], BF16, name="xi_%d" % u, tag="xi", align_bytes=64)
+                xi[u] = xi_tile
+            dst = xi[u][:].rearrange("p (t m j) -> p t m j", t=4, j=4)
+            src = tile[:, :, c0 : c0 + 512].rearrange("p j (m t) -> p t m j", t=4)
+            copy(out=dst[:, t0:t1], in_=src[:, t0:t1])
+
+        def quant_x(u):
+            codes = work.tile([P, 512], U32, name="xq_%d" % u, tag="xq", align_bytes=64)
+            scales = work.tile([P, 512], U8, name="xs_%d" % u, tag="xs", align_bytes=64)
+            nc.vector.quantize_mx(out=codes[:].bitcast(E4M3), scales=scales[:], in_=xi[u][:])
+            xq[u] = (codes, scales)
+
+        def stage1(u, r):
+            b = u // 2
+            bank = psum.tile([P, 4, P], F32, name="h_%d_%d" % (u, r), tag="h%d" % r)
+            codes, scales = xq[u]
+            for t in range(4):
+                nc.tensor.matmul_mx(
+                    out=bank[:, t, :],
+                    lhsT=codes[:, P * t : P * t + P].bitcast(E4M3),
+                    lhsT_scale=scales[:, P * t : P * t + P],
+                    rhs=dop[:, b, 2 * P * r : 2 * P * r + 2 * P].bitcast(E2M1),
+                    rhs_scale=dop_s[:, b, P * r : P * r + P],
+                    start=True,
+                    stop=True,
+                )
+            hb[u, r] = bank
+
+        def gains(u, r):
+            b = u // 2
+            if u not in v:
+                v_tile = work.tile([P, 512, 4], BF16, name="v_%d" % u, tag="v", align_bytes=64)
+                v[u] = v_tile
+            g0 = 512 * b + P * r
+            w = gain[:].bitcast(BF16)[:, g0 : g0 + P].unsqueeze(2).to_broadcast([P, P, 4])
+            dst = v[u][:, P * r : P * r + P, :]
+            src = hb[u, r][:].rearrange("p t n -> p n t")
+            if r < 2:
+                nc.vector.tensor_tensor(out=dst, in0=src, in1=w, op=MULT)
+            else:
+                nc.vector.scalar_tensor_tensor(out=dst, in0=src, scalar=-1.0, in1=w, op0=MULT, op1=MULT)
+
+        def quant_v(u, c0, c1):
+            if u not in vq:
+                v_codes = work.tile([P, 512], U32, name="vq_%d" % u, tag="vq", align_bytes=64)
+                v_scales = work.tile([P, 512], U8, name="vs_%d" % u, tag="vs", align_bytes=64)
+                vq[u] = (v_codes, v_scales)
+            codes, scales = vq[u]
+            nc.vector.quantize_mx(
+                out=codes[:, c0:c1].bitcast(E4M3),
+                scales=scales[:, c0:c1],
+                in_=v[u][:, c0:c1, :].rearrange("p n t -> p (n t)"),
+            )
+
+        def stage2(u, i, branch):
+            b, g = u // 2, u % 2
+            tt, fh = i // 2, i % 2
+            if g == 0 and branch == 0:
+                o_tile = psum.tile([P, 512], F32, name="o_%d_%d" % (b, i), tag="o%d" % i)
+                ob[b, i] = o_tile
+            codes, scales = vq[u]
+            c = T * branch + P * tt
+            f = F * branch + 512 * fh
+            nc.tensor.matmul_mx(
+                out=ob[b, i][:],
+                lhsT=codes[:, c : c + P].bitcast(E4M3),
+                lhsT_scale=scales[:, c : c + P],
+                rhs=dly[b][:, g, 2 * f : 2 * f + 1024].bitcast(E2M1),
+                rhs_scale=dly_s[b][:, g, f : f + 512],
+                start=(g == 0 and branch == 0),
+                stop=(g == 1 and branch == 1),
+            )
+
+        def take_out(b, i, copy):
+            copy(out=res[b][:, i // 2, 512 * (i % 2) : 512 * (i % 2) + 512], in_=ob[b, i][:])
+
+        def store(b, tt):
+            nc.sync.dma_start(out=out[b][P * tt : P * tt + P, :], in_=res[b][:, tt, :])
+
+        def store_half(b, i):
+            tt, f0 = i // 2, 512 * (i % 2)
+            nc.sync.dma_start(
+                out=out[b][P * tt : P * tt + P, f0 : f0 + 512], in_=res[b][:, tt, f0 : f0 + 512]
+            )
+
+        s_copy = nc.scalar.copy
+        v_copy = nc.vector.tensor_copy
+
+        wt = psum.tile([P, P], F32, name="wt", tag="o0")
+        nc.tensor.transpose(wt[:], wrow[:], ident[:])
+        interleave(0, 0, 2, v_copy)
+        interleave(0, 2, 3, v_copy)
+        interleave(0, 3, 4, s_copy)
+        v_copy(out=wcol[:], in_=wt[:, 0 : 2 * G])
+        quant_x(0)
+        wb = []
+        for k in range(2):
+            wb_tile = psum.tile([P, 512], F32, name="wb%d" % k, tag="o%d" % (k + 1))
+            for m in range(4):
+                c = 4 * k + m
+                nc.tensor.transpose(
+                    wb_tile[:, P * m : P * m + P], wcol[:, c : c + 1].to_broadcast([P, P]), ident[:]
+                )
+            wb.append(wb_tile)
+        s_copy(out=gain[:, 0:512], in_=wb[0][:])
+        for r in range(4):
+            stage1(0, r)
+        interleave(1, 0, 2, v_copy)
+        interleave(1, 2, 4, s_copy)
+        interleave(2, 0, 2, s_copy)
+        interleave(2, 2, 4, s_copy)
+        s_copy(out=gain[:, 512:1024], in_=wb[1][:])
+
+        for s in range(UNITS):
+            if s == 0:
+                gains(0, 0)
+                gains(0, 1)
+                quant_x(1)
+                stage1(1, 0)
+                stage1(1, 1)
+                gains(0, 2)
+                stage1(1, 2)
+                gains(0, 3)
+                stage1(1, 3)
+                interleave(3, 0, 2, s_copy)
+                interleave(3, 2, 4, s_copy)
+            else:
+                if s % 2 == 1 and s > 1:
+                    take_out(s // 2 - 1, 2, s_copy)
+                    take_out(s // 2 - 1, 3, s_copy)
+                    store(s // 2 - 1, 1)
+                for i in range(4):
+                    gains(s, i)
+                    if s == UNITS - 1 and i == 2:
+                        quant_v(s, 0, 256)
+                    stage2(s - 1, i, 0)
+                    stage2(s - 1, i, 1)
+                    if s + 1 < UNITS:
+                        stage1(s + 1, i)
+                b = (s - 1) // 2
+                if s % 2 == 0:
+                    if s + 3 < UNITS:
+                        interleave(s + 3, 0, 2, s_copy)
+                    take_out(b, 0, s_copy)
+                    take_out(b, 1, s_copy)
+                    store(b, 0)
+                    if s + 3 < UNITS:
+                        interleave(s + 3, 2, 4, s_copy)
+                else:
+                    if s + 3 < UNITS:
+                        interleave(s + 3, 0, 2, s_copy)
+                        interleave(s + 3, 2, 4, s_copy)
+            if s + 2 < UNITS:
+                quant_x(s + 2)
+            if s < UNITS - 1:
+                quant_v(s, 0, 512)
+            else:
+                quant_v(s, 256, 512)
+
+        last = UNITS - 1
+        for i in range(4):
+            stage2(last, i, 0)
+        for i in range(4):
+            stage2(last, i, 1)
+            take_out(G - 1, i, s_copy if i % 2 == 0 else v_copy)
+            store_half(G - 1, i)

@@ -55,7 +55,7 @@ def tile_real_delay_doppler_expansion_s14_kernel(
         nc.vector.memset(dly_s[0][:].rearrange("p g n -> p (g n)").bitcast(I32), 0)
         make_identity(nc, ident[:])
         for b in range(1, G):
-            nc.gpsimd.memset(dly_s[b][:].rearrange("p g n -> p (g n)").bitcast(I32), 0)
+            nc.vector.memset(dly_s[b][:].rearrange("p g n -> p (g n)").bitcast(I32), 0)
 
         nc.scalar.dma_start(
             out=wrow[0 : 2 * G, :],
@@ -63,7 +63,7 @@ def tile_real_delay_doppler_expansion_s14_kernel(
         )
         ds = doppler_scales.bitcast(I32).rearrange("g (q r) n -> r q g n", r=4)
         for r in range(4):
-            nc.scalar.dma_start(out=dop_s[r:P:32, :, :].bitcast(I32), in_=ds[r])
+            nc.scalar.dma_start(out=dop_s[r:P:32, 0:1, :].bitcast(I32), in_=ds[r][:, 0:1])
         nc.scalar.copy(out=dummy[:, 1:2], in_=dummy[:, 0:1])
 
         def load_x(u):
@@ -93,6 +93,8 @@ def tile_real_delay_doppler_expansion_s14_kernel(
         load_dop(0)
         load_x(1)
         load_x(2)
+        for r in range(4):
+            nc.sync.dma_start(out=dop_s[r:P:32, 1:G, :].bitcast(I32), in_=ds[r][:, 1:G])
         load_dly_s(0)
         load_dly(0, 0)
         load_x(3)
@@ -117,14 +119,14 @@ def tile_real_delay_doppler_expansion_s14_kernel(
         hb = {}
         ob = {}
 
-        def interleave(u, t0, t1, copy):
+        def interleave(u, m0, m1, copy):
             tile, c0 = raw[u]
             if u not in xi:
                 xi_tile = work.tile([P, 2048], BF16, name="xi_%d" % u, tag="xi", align_bytes=64)
                 xi[u] = xi_tile
-            dst = xi[u][:].rearrange("p (t m j) -> p t m j", t=4, j=4)
-            src = tile[:, :, c0 : c0 + 512].rearrange("p j (m t) -> p t m j", t=4)
-            copy(out=dst[:, t0:t1], in_=src[:, t0:t1])
+            dst = xi[u][:].rearrange("p (t m j) -> p m j t", t=4, j=4)
+            src = tile[:, :, c0 : c0 + 512].rearrange("p j (m t) -> p m j t", t=4)
+            copy(out=dst[:, m0:m1], in_=src[:, m0:m1])
 
         def quant_x(u):
             codes = work.tile([P, 512], U32, name="xq_%d" % u, tag="xq", align_bytes=64)
@@ -210,9 +212,8 @@ def tile_real_delay_doppler_expansion_s14_kernel(
 
         wt = psum.tile([P, P], F32, name="wt", tag="o0")
         nc.tensor.transpose(wt[:], wrow[:], ident[:])
-        interleave(0, 0, 2, v_copy)
-        interleave(0, 2, 3, v_copy)
-        interleave(0, 3, 4, s_copy)
+        interleave(0, 0, 96, v_copy)
+        interleave(0, 96, 128, s_copy)
         v_copy(out=wcol[:], in_=wt[:, 0 : 2 * G])
         quant_x(0)
         wb = []
@@ -227,62 +228,47 @@ def tile_real_delay_doppler_expansion_s14_kernel(
         s_copy(out=gain[:, 0:512], in_=wb[0][:])
         for r in range(4):
             stage1(0, r)
-        interleave(1, 0, 2, v_copy)
-        interleave(1, 2, 4, s_copy)
-        interleave(2, 0, 2, s_copy)
-        interleave(2, 2, 4, s_copy)
+        interleave(1, 64, 128, s_copy)
         s_copy(out=gain[:, 512:1024], in_=wb[1][:])
 
         for s in range(UNITS):
+            last = s == UNITS - 1
+            if s % 2 == 1 and s > 1:
+                take_out(s // 2 - 1, 2, s_copy)
+                take_out(s // 2 - 1, 3, s_copy)
+                store(s // 2 - 1, 1)
+            if s + 2 < UNITS:
+                interleave(s + 2, 0, 64, s_copy)
+                interleave(s + 2, 64, 128, s_copy)
+            gains(s, 0)
             if s == 0:
-                gains(0, 0)
-                gains(0, 1)
-                quant_x(1)
-                stage1(1, 0)
-                stage1(1, 1)
-                gains(0, 2)
-                stage1(1, 2)
-                gains(0, 3)
-                stage1(1, 3)
-                interleave(3, 0, 2, s_copy)
-                interleave(3, 2, 4, s_copy)
+                interleave(1, 0, 64, v_copy)
             else:
-                if s % 2 == 1 and s > 1:
-                    take_out(s // 2 - 1, 2, s_copy)
-                    take_out(s // 2 - 1, 3, s_copy)
-                    store(s // 2 - 1, 1)
-                for i in range(4):
-                    gains(s, i)
-                    if s == UNITS - 1 and i == 2:
-                        quant_v(s, 0, 256)
+                quant_v(s - 1, 0, 512)
+            gains(s, 1)
+            if not last:
+                quant_x(s + 1)
+            gains(s, 2)
+            if last:
+                quant_v(s, 0, 256)
+            gains(s, 3)
+            for i in range(4):
+                if s > 0:
                     stage2(s - 1, i, 0)
                     stage2(s - 1, i, 1)
-                    if s + 1 < UNITS:
-                        stage1(s + 1, i)
-                b = (s - 1) // 2
-                if s % 2 == 0:
-                    if s + 3 < UNITS:
-                        interleave(s + 3, 0, 2, s_copy)
-                    take_out(b, 0, s_copy)
-                    take_out(b, 1, s_copy)
-                    store(b, 0)
-                    if s + 3 < UNITS:
-                        interleave(s + 3, 2, 4, s_copy)
-                else:
-                    if s + 3 < UNITS:
-                        interleave(s + 3, 0, 2, s_copy)
-                        interleave(s + 3, 2, 4, s_copy)
-            if s + 2 < UNITS:
-                quant_x(s + 2)
-            if s < UNITS - 1:
-                quant_v(s, 0, 512)
-            else:
-                quant_v(s, 256, 512)
+                if not last and i > 0:
+                    stage1(s + 1, i - 1)
+            if not last:
+                stage1(s + 1, 3)
+            if s % 2 == 0 and s > 0:
+                take_out(s // 2 - 1, 0, s_copy)
+                take_out(s // 2 - 1, 1, s_copy)
+                store(s // 2 - 1, 0)
+        quant_v(UNITS - 1, 256, 512)
 
-        last = UNITS - 1
         for i in range(4):
-            stage2(last, i, 0)
+            stage2(UNITS - 1, i, 0)
         for i in range(4):
-            stage2(last, i, 1)
+            stage2(UNITS - 1, i, 1)
             take_out(G - 1, i, s_copy if i % 2 == 0 else v_copy)
             store_half(G - 1, i)

@@ -31,7 +31,7 @@ def tile_real_delay_doppler_expansion_s14_kernel(
 
         raw = []
         for u in range(UNITS):
-            if u < 4:
+            if u < 2:
                 raw_half = keep.tile([P, 4, 512], BF16, name="raw%d" % u, align_bytes=64)
                 raw.append((raw_half, 0))
             elif u % 2 == 0:
@@ -69,7 +69,7 @@ def tile_real_delay_doppler_expansion_s14_kernel(
         def load_x(u):
             tile, c0 = raw[u]
             b = u // 2
-            if u < 4:
+            if u < 2:
                 src = x[b][:, 512 * (u % 2) : 512 * (u % 2) + 512]
             else:
                 src = x[b]
@@ -97,10 +97,9 @@ def tile_real_delay_doppler_expansion_s14_kernel(
             nc.sync.dma_start(out=dop_s[r:P:32, 1:G, :].bitcast(I32), in_=ds[r][:, 1:G])
         load_dly_s(0)
         load_dly(0, 0)
-        load_x(3)
+        load_x(4)
         load_dly(0, 1)
         load_dop(2)
-        load_x(4)
         load_dly_s(1)
         load_dly(1, 0)
         load_dly(1, 1)
@@ -212,10 +211,7 @@ def tile_real_delay_doppler_expansion_s14_kernel(
 
         wt = psum.tile([P, P], F32, name="wt", tag="o0")
         nc.tensor.transpose(wt[:], wrow[:], ident[:])
-        interleave(0, 0, 96, v_copy)
-        interleave(0, 96, 128, s_copy)
-        v_copy(out=wcol[:], in_=wt[:, 0 : 2 * G])
-        quant_x(0)
+        s_copy(out=wcol[:], in_=wt[:, 0 : 2 * G])
         wb = []
         for k in range(2):
             wb_tile = psum.tile([P, 512], F32, name="wb%d" % k, tag="o%d" % (k + 1))
@@ -225,50 +221,65 @@ def tile_real_delay_doppler_expansion_s14_kernel(
                     wb_tile[:, P * m : P * m + P], wcol[:, c : c + 1].to_broadcast([P, P]), ident[:]
                 )
             wb.append(wb_tile)
+        interleave(0, 0, 88, v_copy)
+        interleave(0, 88, 128, s_copy)
+        quant_x(0)
         s_copy(out=gain[:, 0:512], in_=wb[0][:])
         for r in range(4):
             stage1(0, r)
-        interleave(1, 64, 128, s_copy)
+        interleave(1, 40, 128, s_copy)
         s_copy(out=gain[:, 512:1024], in_=wb[1][:])
+        interleave(2, 0, 128, s_copy)
 
         for s in range(UNITS):
             last = s == UNITS - 1
-            if s % 2 == 1 and s > 1:
-                take_out(s // 2 - 1, 2, s_copy)
-                take_out(s // 2 - 1, 3, s_copy)
-                store(s // 2 - 1, 1)
-            if s + 2 < UNITS:
-                interleave(s + 2, 0, 64, s_copy)
-                interleave(s + 2, 64, 128, s_copy)
             gains(s, 0)
             if s == 0:
-                interleave(1, 0, 64, v_copy)
+                interleave(1, 0, 40, v_copy)
+            elif last:
+                quant_v(s - 1, 256, 512)
             else:
                 quant_v(s - 1, 0, 512)
-            gains(s, 1)
             if not last:
+                gains(s, 1)
                 quant_x(s + 1)
-            gains(s, 2)
-            if last:
-                quant_v(s, 0, 256)
-            gains(s, 3)
+                gains(s, 2)
+                if s == UNITS - 2:
+                    quant_v(s, 0, 256)
+                gains(s, 3)
+            else:
+                gains(s, 2)
+                quant_v(s, 0, 128)
+                gains(s, 1)
+                quant_v(s, 256, 384)
+                gains(s, 3)
+                quant_v(s, 128, 256)
+                quant_v(s, 384, 512)
+            if (s % 2 == 1 or s == 0) and s + 3 < UNITS:
+                interleave(s + 3, 0, 128, s_copy)
             for i in range(4):
-                if s > 0:
+                if last:
+                    stage2(s - 1, i, 0)
+                elif s > 0:
                     stage2(s - 1, i, 0)
                     stage2(s - 1, i, 1)
                 if not last and i > 0:
                     stage1(s + 1, i - 1)
             if not last:
                 stage1(s + 1, 3)
+            else:
+                for i in range(4):
+                    stage2(s - 1, i, 1)
             if s % 2 == 0 and s > 0:
-                take_out(s // 2 - 1, 0, s_copy)
-                take_out(s // 2 - 1, 1, s_copy)
-                store(s // 2 - 1, 0)
-        quant_v(UNITS - 1, 256, 512)
+                for i in range(4):
+                    take_out(s // 2 - 1, i, s_copy)
+                    if i % 2 == 1:
+                        store(s // 2 - 1, i // 2)
+                if s + 3 < UNITS:
+                    interleave(s + 3, 0, 128, s_copy)
 
         for i in range(4):
             stage2(UNITS - 1, i, 0)
-        for i in range(4):
             stage2(UNITS - 1, i, 1)
             take_out(G - 1, i, s_copy if i % 2 == 0 else v_copy)
             store_half(G - 1, i)

from contextlib import ExitStack

import concourse.mybir as mybir
from concourse.masks import make_identity

G, K, L, T, F = 4, 512, 1024, 256, 1024
FLOPS = 2 * G * (2 * T * K * L + T * F * 2 * L)

F32 = mybir.dt.float32
BF16 = mybir.dt.bfloat16
U32 = mybir.dt.uint32
I32 = mybir.dt.int32
U8 = mybir.dt.uint8
E4M3 = mybir.dt.float8_e4m3fn_x4
E2M1 = mybir.dt.float4_e2m1fn_x4
MULT = mybir.AluOpType.mult

P = 128
UNITS = 2 * G


def tile_real_delay_doppler_expansion_s14_kernel(
    tc, x, doppler_words, doppler_scales, window, delay_words, delay_scales, out
):
    nc = tc.nc
    with ExitStack() as ctx:
        keep = ctx.enter_context(tc.tile_pool(name="keep", bufs=1))
        work = ctx.enter_context(tc.tile_pool(name="work", bufs=3))
        psum = ctx.enter_context(tc.psum_pool(name="psum", bufs=1))
        ctx.enter_context(tc.manual_schedule())

        raw = []
        for u in range(UNITS):
            if u < 2:
                raw_half = keep.tile([P, 4, 512], BF16, name="raw%d" % u, align_bytes=64)
                raw.append((raw_half, 0))
            elif u % 2 == 0:
                raw_band = keep.tile([P, 4, L], BF16, name="raw%d" % u, align_bytes=64)
                raw.append((raw_band, 0))
                raw.append((raw_band, 512))
        dop = keep.tile([P, G, 4 * T], U8, name="dop", align_bytes=64)
        dop_s = keep.tile([P, G, 2 * T], U8, name="dop_s", align_bytes=64)
        dly = [keep.tile([P, 2, 4 * F], U8, name="dly%d" % b, align_bytes=64) for b in range(G)]
        dly_s = [keep.tile([P, 2, 2 * F], U8, name="dly_s%d" % b, align_bytes=64) for b in range(G)]
        res = [keep.tile([P, 2, F], F32, name="res%d" % b, align_bytes=64) for b in range(G)]
        ident = keep.tile([P, P], F32, name="ident", align_bytes=64)
        wrow = keep.tile([P, P], F32, name="wrow", align_bytes=64)
        wcol = keep.tile([P, 2 * G], F32, name="wcol", align_bytes=64)
        gain = keep.tile([P, G * T], F32, name="gain", align_bytes=64)
        dummy = keep.tile([P, 2], BF16, name="dummy", align_bytes=64)

        nc.vector.memset(wrow[:], 0.0)
        nc.vector.memset(dop_s[:].rearrange("p g n -> p (g n)").bitcast(I32), 0)
        nc.vector.memset(dummy[:], 0.0)
        nc.vector.memset(dly_s[0][:].rearrange("p g n -> p (g n)").bitcast(I32), 0)
        make_identity(nc, ident[:])
        for b in range(1, G):
            nc.vector.memset(dly_s[b][:].rearrange("p g n -> p (g n)").bitcast(I32), 0)

        nc.scalar.dma_start(
            out=wrow[0 : 2 * G, :],
            in_=window.bitcast(F32).rearrange("b (h n) -> (b h) n", h=2),
        )
        ds = doppler_scales.bitcast(I32).rearrange("g (q r) n -> r q g n", r=4)
        for r in range(4):
            nc.scalar.dma_start(out=dop_s[r:P:32, 0:1, :].bitcast(I32), in_=ds[r][:, 0:1])
        nc.scalar.copy(out=dummy[:, 1:2], in_=dummy[:, 0:1])

        def load_x(u):
            tile, c0 = raw[u]
            b = u // 2
            if u < 2:
                src = x[b][:, 512 * (u % 2) : 512 * (u % 2) + 512]
            else:
                src = x[b]
            nc.sync.dma_start(out=tile[:], in_=src.rearrange("(p j) l -> p j l", j=4))

        def load_dop(b0):
            nc.sync.dma_start(
                out=dop[:, b0 : b0 + 2, :],
                in_=doppler_words[b0 : b0 + 2].rearrange("g p c -> p g c"),
            )

        def load_dly(b, g):
            nc.sync.dma_start(out=dly[b][:, g, :], in_=delay_words[2 * b + g])

        def load_dly_s(b):
            src = delay_scales[2 * b : 2 * b + 2].bitcast(I32).rearrange("g (q r) n -> r q g n", r=4)
            for r in range(4):
                nc.sync.dma_start(out=dly_s[b][r:P:32, :, :].bitcast(I32), in_=src[r])

        load_x(0)
        load_dop(0)
        load_x(1)
        load_x(2)
        for r in range(4):
            nc.sync.dma_start(out=dop_s[r:P:32, 1:G, :].bitcast(I32), in_=ds[r][:, 1:G])
        load_dly_s(0)
        load_dly(0, 0)
        load_x(4)
        load_dly(0, 1)
        load_dop(2)
        load_dly_s(1)
        load_dly(1, 0)
        load_dly(1, 1)
        load_x(6)
        load_dly_s(2)
        load_dly(2, 0)
        load_dly(2, 1)
        load_dly_s(3)
        load_dly(3, 0)
        load_dly(3, 1)

        xi = {}
        xq = {}
        v = {}
        vq = {}
        hb = {}
        ob = {}

        def interleave(u, m0, m1, copy):
            tile, c0 = raw[u]
            if u not in xi:
                xi_tile = work.tile([P, 2048], BF16, name="xi_%d" % u, tag="xi", align_bytes=64)
                xi[u] = xi_tile
            dst = xi[u][:].rearrange("p (t m j) -> p m j t", t=4, j=4)
            src = tile[:, :, c0 : c0 + 512].rearrange("p j (m t) -> p m j t", t=4)
            copy(out=dst[:, m0:m1], in_=src[:, m0:m1])

        def quant_x(u):
            codes = work.tile([P, 512], U32, name="xq_%d" % u, tag="xq", align_bytes=64)
            scales = work.tile([P, 512], U8, name="xs_%d" % u, tag="xs", align_bytes=64)
            nc.vector.quantize_mx(out=codes[:].bitcast(E4M3), scales=scales[:], in_=xi[u][:])
            xq[u] = (codes, scales)

        def stage1(u, r):
            b = u // 2
            bank = psum.tile([P, 4, P], F32, name="h_%d_%d" % (u, r), tag="h%d" % r)
            codes, scales = xq[u]
            for t in range(4):
                nc.tensor.matmul_mx(
                    out=bank[:, t, :],
                    lhsT=codes[:, P * t : P * t + P].bitcast(E4M3),
                    lhsT_scale=scales[:, P * t : P * t + P],
                    rhs=dop[:, b, 2 * P * r : 2 * P * r + 2 * P].bitcast(E2M1),
                    rhs_scale=dop_s[:, b, P * r : P * r + P],
                    start=True,
                    stop=True,
                )
            hb[u, r] = bank

        def gains(u, r):
            b = u // 2
            if u not in v:
                v_tile = work.tile([P, 512, 4], BF16, name="v_%d" % u, tag="v", align_bytes=64)
                v[u] = v_tile
            g0 = 512 * b + P * r
            w = gain[:].bitcast(BF16)[:, g0 : g0 + P].unsqueeze(2).to_broadcast([P, P, 4])
            dst = v[u][:, P * r : P * r + P, :]
            src = hb[u, r][:].rearrange("p t n -> p n t")
            if r < 2:
                nc.vector.tensor_tensor(out=dst, in0=src, in1=w, op=MULT)
            else:
                nc.vector.scalar_tensor_tensor(out=dst, in0=src, scalar=-1.0, in1=w, op0=MULT, op1=MULT)

        def quant_v(u, c0, c1):
            if u not in vq:
                v_codes = work.tile([P, 512], U32, name="vq_%d" % u, tag="vq", align_bytes=64)
                v_scales = work.tile([P, 512], U8, name="vs_%d" % u, tag="vs", align_bytes=64)
                vq[u] = (v_codes, v_scales)
            codes, scales = vq[u]
            nc.vector.quantize_mx(
                out=codes[:, c0:c1].bitcast(E4M3),
                scales=scales[:, c0:c1],
                in_=v[u][:, c0:c1, :].rearrange("p n t -> p (n t)"),
            )

        def stage2(u, i, branch):
            b, g = u // 2, u % 2
            tt, fh = i // 2, i % 2
            if g == 0 and branch == 0:
                o_tile = psum.tile([P, 512], F32, name="o_%d_%d" % (b, i), tag="o%d" % i)
                ob[b, i] = o_tile
            codes, scales = vq[u]
            c = T * branch + P * tt
            f = F * branch + 512 * fh
            nc.tensor.matmul_mx(
                out=ob[b, i][:],
                lhsT=codes[:, c : c + P].bitcast(E4M3),
                lhsT_scale=scales[:, c : c + P],
                rhs=dly[b][:, g, 2 * f : 2 * f + 1024].bitcast(E2M1),
                rhs_scale=dly_s[b][:, g, f : f + 512],
                start=(g == 0 and branch == 0),
                stop=(g == 1 and branch == 1),
            )

        def take_out(b, i, copy):
            copy(out=res[b][:, i // 2, 512 * (i % 2) : 512 * (i % 2) + 512], in_=ob[b, i][:])

        def store(b, tt):
            nc.sync.dma_start(out=out[b][P * tt : P * tt + P, :], in_=res[b][:, tt, :])

        def store_half(b, i):
            tt, f0 = i // 2, 512 * (i % 2)
            nc.sync.dma_start(
                out=out[b][P * tt : P * tt + P, f0 : f0 + 512], in_=res[b][:, tt, f0 : f0 + 512]
            )

        s_copy = nc.scalar.copy
        v_copy = nc.vector.tensor_copy

        wt = psum.tile([P, P], F32, name="wt", tag="o0")
        nc.tensor.transpose(wt[:], wrow[:], ident[:])
        s_copy(out=wcol[:], in_=wt[:, 0 : 2 * G])
        wb = []
        for k in range(2):
            wb_tile = psum.tile([P, 512], F32, name="wb%d" % k, tag="o%d" % (k + 1))
            for m in range(4):
                c = 4 * k + m
                nc.tensor.transpose(
                    wb_tile[:, P * m : P * m + P], wcol[:, c : c + 1].to_broadcast([P, P]), ident[:]
                )
            wb.append(wb_tile)
        interleave(0, 0, 88, v_copy)
        interleave(0, 88, 128, s_copy)
        quant_x(0)
        s_copy(out=gain[:, 0:512], in_=wb[0][:])
        for r in range(4):
            stage1(0, r)
        interleave(1, 40, 128, s_copy)
        s_copy(out=gain[:, 512:1024], in_=wb[1][:])
        interleave(2, 0, 128, s_copy)

        for s in range(UNITS):
            last = s == UNITS - 1
            gains(s, 0)
            if s == 0:
                interleave(1, 0, 40, v_copy)
            elif last:
                quant_v(s - 1, 256, 512)
            else:
                quant_v(s - 1, 0, 512)
            if not last:
                gains(s, 1)
                quant_x(s + 1)
                gains(s, 2)
                if s == UNITS - 2:
                    quant_v(s, 0, 256)
                gains(s, 3)
            else:
                gains(s, 2)
                quant_v(s, 0, 128)
                gains(s, 1)
                quant_v(s, 256, 384)
                gains(s, 3)
                quant_v(s, 128, 256)
                quant_v(s, 384, 512)
            if (s % 2 == 1 or s == 0) and s + 3 < UNITS:
                interleave(s + 3, 0, 128, s_copy)
            for i in range(4):
                if last:
                    stage2(s - 1, i, 0)
                elif s > 0:
                    stage2(s - 1, i, 0)
                    stage2(s - 1, i, 1)
                if not last and i > 0:
                    stage1(s + 1, i - 1)
            if not last:
                stage1(s + 1, 3)
            else:
                for i in range(4):
                    stage2(s - 1, i, 1)
            if s % 2 == 0 and s > 0:
                for i in range(4):
                    take_out(s // 2 - 1, i, s_copy)
                    if i % 2 == 1:
                        store(s // 2 - 1, i // 2)
                if s + 3 < UNITS:
                    interleave(s + 3, 0, 128, s_copy)

        for i in range(4):
            stage2(UNITS - 1, i, 0)
            stage2(UNITS - 1, i, 1)
            take_out(G - 1, i, s_copy if i % 2 == 0 else v_copy)
            store_half(G - 1, i)
